import numpy as np
import ml_dtypes


def mxq(x, axis, fmt="e4m3"):
    dtype, down = {"e4m3": (ml_dtypes.float8_e4m3fn, 7), "e5m2": (ml_dtypes.float8_e5m2, 14)}[fmt]
    v = np.moveaxis(np.asarray(x, np.float32).astype(ml_dtypes.bfloat16).astype(np.float64), axis, -1)
    blocks = v.reshape(v.shape[:-1] + (-1, 32))
    amax = np.abs(blocks).max(-1, keepdims=True)
    byte = np.maximum(np.where(amax > 0, np.frexp(amax)[1] - 1 + 127, 0) - down, 1)
    scale = np.exp2(byte - 127.0)
    codes = (blocks / scale).astype(np.float32).astype(dtype).astype(np.float64)
    return np.moveaxis((codes * scale).reshape(v.shape), -1, axis)


WIDE = False


def mx_kscale(k):
    if not WIDE:
        return np.ones(k)
    levels = np.array([10, -10, 5, -5, 0])
    if k % 512:
        return np.exp2(np.random.permutation(np.resize(levels, k // 32))).repeat(32)
    a = np.empty((k // 512, 16))
    for p in range(k // 512):
        a[p, :8] = np.random.permutation(np.resize(levels, 8))
        for g in range(8):
            far = levels[np.abs(levels - a[p, g]) >= 10]
            a[p, g + 8] = far[np.random.randint(len(far))]
    return np.exp2(a.ravel()).repeat(32)


def f64(x):
    return np.asarray(x).astype(np.float64)


def striped(idx):
    return np.tile(idx.reshape(-1, 16).T, (8, 1)).astype(np.uint16)


def unstriped(offs):
    return offs[:16].T.reshape(-1).astype(np.int64)


def pack_weight(w):
    k, n = w.shape
    w = f64(np.asarray(w, np.float32).astype(ml_dtypes.bfloat16)).reshape(k // 32, 32, n)
    amax = np.abs(w).max(1)
    byte = np.clip(np.where(amax > 0, np.frexp(amax)[1] - 1 + 127 - 7, 1), 1, 254)
    scaled = (w * np.exp2(127.0 - byte)[:, None, :]).reshape(k, n).astype(np.float32)
    words = np.ascontiguousarray(scaled.reshape(k // 512, 128, 4, n).transpose(0, 1, 3, 2)).astype(ml_dtypes.float8_e4m3fn).view(np.uint8)
    return words, np.ascontiguousarray(byte.astype(np.uint8).reshape(k // 512, 16, n))


def unpack_weight(words, scales):
    g, p, n, _ = words.shape
    vals = np.ascontiguousarray(words).view(ml_dtypes.float8_e4m3fn).astype(np.float64) * np.repeat(np.exp2(scales.astype(np.float64) - 127.0), 8, axis=1)[..., None]
    return vals.transpose(0, 1, 3, 2).reshape(g * 512, n)


def sigmoid(v):
    return 1.0 / (1.0 + np.exp(-np.maximum(v, -700.0)))


K, T, S, N, H, W = 512, 2048, 512, 512, 512, 256


def setup_inputs():
    n = np.random.standard_normal
    s = mx_kscale(K)[:, None]
    u = mx_kscale(S)
    packed_xT = pack_weight(n((K, T)) * s)
    perm = np.random.permutation(N)
    return {
        "x_words": packed_xT[0],
        "x_scales": packed_xT[1],
        "wa": (n((K, H)) / np.sqrt(K) / s).astype(np.float32),
        "wb": (n((K, N)) / np.sqrt(K) / s).astype(np.float32),
        "gt": (np.random.uniform(0.5, 1.5, (S, 1)) * u[:, None]).astype(np.float32),
        "gi": (np.random.uniform(0.5, 1.5, (S, 1)) / u[:, None]).astype(np.float32),
        "sl": np.random.uniform(1.0, 2.0, (H, 1)).astype(np.float32),
        "th": (0.5 * n((H, 1))).astype(np.float32),
        "offs": striped(np.random.permutation(T)[:S]),
        "two": striped(np.random.permutation(T)[:S]),
        "n1": striped(np.random.permutation(H)),
        "n2": striped(np.random.permutation(H)),
        "n3": striped(perm[:W]),
        "n4": striped(perm[W:]),
    }


def reference(x_words, x_scales, wa, wb, gt, gi, sl, th, offs, two, n1, n2, n3, n4):
    xq = unpack_weight(x_words, x_scales)[:, unstriped(offs)]
    a = xq.T @ mxq(f64(wa), 0, "e4m3")
    pa = a[:, unstriped(n1)]
    pb = a[:, unstriped(n2)]
    z = f64(gt) * (np.maximum(np.minimum(a, pa), np.minimum(np.maximum(a, pa), pb)))
    x_two = unpack_weight(x_words, x_scales)[:, unstriped(two)]
    b = x_two.T @ mxq(f64(wb), 0, "e4m3")
    z2 = f64(gi) * b
    cv = 0.0625 * ((mxq(z, 0, "e4m3").T @ mxq(z2, 0, "e4m3")))
    pb2 = cv[:, unstriped(n4)]
    sg = sigmoid(f64(sl) * (cv[:, unstriped(n3)] - f64(th)))
    rb = pb2 - sg
    pa2 = cv[:, unstriped(n3)]
    sg2 = sigmoid(f64(sl) * (cv[:, unstriped(n4)] - f64(th)))
    ra = pa2 * sg2
    ds = np.zeros((H, N))
    ds[:, unstriped(n3)] = ra
    out = ds.copy()
    out[:, unstriped(n4)] = rb
    return out

@@ -1,0 +1,210 @@
+from contextlib import ExitStack
+
+import concourse.mybir as mybir
+
+K, T, S, H, N, W = 512, 2048, 512, 512, 512, 256
+FLOPS = 2 * S * K * H + 2 * S * K * N + 2 * H * S * N
+
+F32 = mybir.dt.float32
+BF16 = mybir.dt.bfloat16
+I32 = mybir.dt.int32
+U32 = mybir.dt.uint32
+U16 = mybir.dt.uint16
+U8 = mybir.dt.uint8
+FP8X4 = mybir.dt.float8_e4m3fn_x4
+ALU = mybir.AluOpType
+ACT = mybir.ActivationFunctionType
+
+P = 128
+PACK = 4
+RUN = 8
+HALF = 256
+BLOCKS = 4
+LIST_COLS = P // 16
+
+
+def tile_picked_mommedeod_none_p_kernel(tc, x_words, x_scales, wa, wb, gt, gi, sl, th, offs, two, n1, n2, n3, n4, out):
+    nc = tc.nc
+    with ExitStack() as ctx:
+        lists = ctx.enter_context(tc.tile_pool(name="lists", bufs=1))
+        keep = ctx.enter_context(tc.tile_pool(name="keep", bufs=1))
+        psum = ctx.enter_context(tc.psum_pool(name="psum", bufs=1))
+
+        def load_list(name, src):
+            t = lists.tile(list(src.shape), U16, name=name)
+            nc.sync.dma_start(t[:], src)
+            return t
+
+        def load_half(name, w, h):
+            raw = keep.tile([P, PACK, HALF], F32, name=name)
+            nc.sync.dma_start(raw[:], w[:, h * HALF : (h + 1) * HALF].rearrange("(p j) n -> p j n", j=PACK))
+            return raw
+
+        offs_t = load_list("offs_t", offs)
+        two_t = load_list("two_t", two)
+        xs = keep.tile([P, T], U8, name="xs")
+        for q in range(4):
+            rows4 = x_scales[0, 4 * q : 4 * q + 4, :].bitcast(I32)
+            nc.sync.dma_start(xs[32 * q : 32 * q + 32, :].bitcast(I32), rows4.unsqueeze(0).to_broadcast([8, 4, T // 4]))
+        xw = keep.tile([P, T], I32, name="xw")
+        nc.sync.dma_start(xw[:], x_words[0].rearrange("p n t -> p (n t)").bitcast(I32))
+        wa_raw = [load_half("wa_raw%d" % h, wa, h) for h in range(2)]
+        wb_raw = [load_half("wb_raw%d" % h, wb, h) for h in range(2)]
+        n1_t = load_list("n1_t", n1)
+        n2_t = load_list("n2_t", n2)
+
+        gt_t = keep.tile([P, PACK, 8], F32, name="gt_t")
+        gi_t = keep.tile([P, PACK, 8], F32, name="gi_t")
+        sl_t = keep.tile([P, BLOCKS], F32, name="sl_t")
+        th_t = keep.tile([P, BLOCKS], F32, name="th_t")
+        with nc.allow_non_contiguous_dma(reason="one value a partition and column"):
+            for dst, src, queue in ((gt_t, gt, nc.gpsimd), (gi_t, gi, nc.sync)):
+                for t in range(PACK):
+                    queue.dma_start(dst[:, t, 0:1], src.rearrange("(q t r) o -> t q r o", t=PACK, r=RUN)[t])
+            nc.gpsimd.dma_start(sl_t[:], sl.rearrange("(c p) o -> p (c o)", p=P))
+            nc.gpsimd.dma_start(th_t[:], th.rearrange("(c p) o -> p (c o)", p=P))
+        n3_t = load_list("n3_t", n3)
+        n4_t = load_list("n4_t", n4)
+        slth = keep.tile([P, BLOCKS], F32, name="slth")
+        bias_t = keep.tile([P, BLOCKS], F32, name="bias_t")
+        nc.gpsimd.tensor_tensor(slth[:], sl_t[:], th_t[:], ALU.mult)
+        nc.gpsimd.tensor_scalar(bias_t[:], slth[:], -1.0, 0.0, ALU.mult, ALU.add)
+
+        def pick(name, window, offsets, dtype, tag=None):
+            g = keep.tile([P, PACK, P], dtype, name=name, tag=tag or name, align_bytes=64)
+            nc.vector.tensor_copy(g[:].rearrange("p t (q r) -> p q t r", r=RUN), window.indirect(offsets[:]))
+            return g
+
+        def interleaved(t):
+            return t.rearrange("p (c i) t -> p c t i", i=4)
+
+        def planes(t):
+            return t.rearrange("p t (c i) -> p c t i", i=4)
+
+        def round_weights(name, raw, copy):
+            g = keep.tile([P, HALF, PACK], BF16, name=name, tag=name, align_bytes=64)
+            copy(interleaved(g[:]), planes(raw[:]))
+            return g
+
+        def gpsimd_round(dst, src):
+            nc.gpsimd.tensor_scalar(dst, src, 1.0, 0.0, ALU.mult, ALU.add)
+
+        def quantise(codes, scales, grouped):
+            nc.vector.quantize_mx(out=codes.bitcast(FP8X4), scales=scales, in_=grouped.rearrange("p n t -> p (n t)"))
+
+        xa_s = pick("xa_s", xs[:], offs_t, U8)
+        xa_w = pick("xa_w", xw[:].bitcast(U32), offs_t, U32)
+        xb_s = pick("xb_s", xs[:], two_t, U8)
+
+        wa_codes = [keep.tile([P, HALF], U32, name="wa_codes%d" % h, align_bytes=64) for h in range(2)]
+        wa_scales = [keep.tile([P, HALF], U8, name="wa_scales%d" % h, align_bytes=64) for h in range(2)]
+        wb_codes = [keep.tile([P, HALF], U32, name="wb_codes%d" % h, align_bytes=64) for h in range(2)]
+        wb_scales = [keep.tile([P, HALF], U8, name="wb_scales%d" % h, align_bytes=64) for h in range(2)]
+
+        wa_bf = [round_weights("wa_bf0", wa_raw[0], nc.scalar.copy), round_weights("wa_bf1", wa_raw[1], nc.vector.tensor_copy)]
+        a_ps = [psum.tile([P, H], F32, name="a_ps%d" % t, tag="bank%d" % t) for t in range(PACK)]
+        for h in range(2):
+            quantise(wa_codes[h][:], wa_scales[h][:], wa_bf[h][:])
+        for t in range(PACK):
+            for h in range(2):
+                nc.tensor.matmul_mx(
+                    out=a_ps[t][:, h * HALF : (h + 1) * HALF],
+                    lhsT=xa_w[:, t, :].bitcast(FP8X4), lhsT_scale=xa_s[:, t, :],
+                    rhs=wa_codes[h][:].bitcast(FP8X4), rhs_scale=wa_scales[h][:],
+                    start=True, stop=True,
+                )
+        xb_w = pick("xb_w", xw[:].bitcast(U32), two_t, U32, tag="wa_bf1")
+
+        wb_bf0 = round_weights("wb_bf0", wb_raw[0], nc.scalar.copy)
+        a_sb = keep.tile([P, PACK, H], F32, name="a_sb")
+        for t in range(PACK):
+            if "SSSS"[t] == "S":
+                nc.scalar.activation(a_sb[:, t, :], a_ps[t][:], ACT.Copy, scale=gt_t[:, t, 0:1])
+            else:
+                nc.vector.tensor_scalar(a_sb[:, t, :], a_ps[t][:], gt_t[:, t, 0:1], None, ALU.mult)
+        wb_bf = [wb_bf0, round_weights("wb_bf1", wb_raw[1], nc.vector.tensor_copy)]
+
+        z2_codes = keep.tile([P, N], U32, name="z2_codes", align_bytes=64)
+        z2_scales = keep.tile([P, N], U8, name="z2_scales", align_bytes=64)
+        gi_wide = gi_t[:, :, 0:1].unsqueeze(1).to_broadcast([P, P // 4, PACK, 4])
+        for h in range(2):
+            quantise(wb_codes[h][:], wb_scales[h][:], wb_bf[h][:])
+            z2_bf = keep.tile([P, HALF, PACK], BF16, name="z2_bf%d" % h, align_bytes=64)
+            for u in range(2):
+                b_ps = psum.tile([P, PACK, P], F32, name="b_ps%d" % (2 * h + u), tag="bank%d" % (4 + 2 * h + u))
+                cols = slice(u * P, (u + 1) * P)
+                for t in range(PACK):
+                    nc.tensor.matmul_mx(
+                        out=b_ps[:, t, :],
+                        lhsT=xb_w[:, t, :].bitcast(FP8X4), lhsT_scale=xb_s[:, t, :],
+                        rhs=wb_codes[h][:, cols].bitcast(FP8X4), rhs_scale=wb_scales[h][:, cols],
+                        start=True, stop=True,
+                    )
+                nc.vector.tensor_tensor(interleaved(z2_bf[:, cols, :]), planes(b_ps[:]), gi_wide, ALU.mult)
+            quantise(z2_codes[:, h * HALF : (h + 1) * HALF], z2_scales[:, h * HALF : (h + 1) * HALF], z2_bf[:])
+
+        def fetch(engine, dst, window, offsets):
+            if engine == "scalar":
+                nc.scalar.activation(dst, window.indirect(offsets), ACT.Copy)
+            else:
+                nc.vector.tensor_copy(dst, window.indirect(offsets))
+
+        def moments(c):
+            cols = slice(c * P, (c + 1) * P)
+            entries = slice(c * LIST_COLS, (c + 1) * LIST_COLS)
+
+            pa = keep.tile([P, PACK, P], F32, name="pa%d" % c, tag="lo%d" % (c - 1 if c > 1 else -1 - c), align_bytes=64)
+            pb = keep.tile([P, PACK, P], F32, name="pb%d" % c, tag="z_codes%d" % (c - 1 if c > 1 else -1 - c), align_bytes=64)
+            for t in range(PACK):
+                engine = "scalar" if "SSSSSSSSVVVVVVVV"[c * PACK + t] == "S" else "vector"
+                fetch(engine, pa[:, t, :], a_sb[:, t, :], n1_t[:, entries])
+                fetch(engine, pb[:, t, :], a_sb[:, t, :], n2_t[:, entries])
+            hi = keep.tile([P, PACK, P], F32, name="hi%d" % c, tag="hi%d" % c, align_bytes=64)
+            lo = keep.tile([P, PACK, P], F32, name="lo%d" % c, tag="lo%d" % c, align_bytes=64)
+            mid = keep.tile([P, PACK, P], F32, name="mid%d" % c)
+            step = 4 if c == 0 else PACK
+            for t0 in range(0, PACK, step):
+                ts = slice(t0, t0 + step)
+                nc.vector.tensor_tensor(hi[:, ts, :], pa[:, ts, :], pb[:, ts, :], ALU.max)
+                nc.vector.tensor_tensor(lo[:, ts, :], pa[:, ts, :], pb[:, ts, :], ALU.min)
+                nc.vector.tensor_tensor(mid[:, ts, :], hi[:, ts, :], a_sb[:, ts, cols], ALU.min)
+            z_bf = keep.tile([P, P, PACK], BF16, name="z_bf%d" % c, tag="z_bf%d" % c, align_bytes=64)
+            nc.vector.tensor_tensor(interleaved(z_bf[:]), planes(lo[:]), planes(mid[:]), ALU.max)
+            z_codes = keep.tile([P, P], U32, name="z_codes%d" % c, tag="z_codes%d" % c, align_bytes=64)
+            z_scales = keep.tile([P, P], U8, name="z_scales%d" % c, align_bytes=64)
+            quantise(z_codes[:], z_scales[:], z_bf[:])
+            cv_ps = psum.tile([P, N], F32, name="cv_ps%d" % c, tag="bank%d" % c)
+            nc.tensor.matmul_mx(
+                out=cv_ps[:],
+                lhsT=z_codes[:].bitcast(FP8X4), lhsT_scale=z_scales[:],
+                rhs=z2_codes[:].bitcast(FP8X4), rhs_scale=z2_scales[:],
+                start=True, stop=True,
+            )
+            cv = keep.tile([P, N], F32, name="cv%d" % c)
+            if c < 1:
+                nc.scalar.activation(cv[:], cv_ps[:], ACT.Copy, scale=0.0625)
+            else:
+                nc.vector.tensor_scalar(cv[:], cv_ps[:], 0.0625, None, ALU.mult)
+            return cv
+
+        def pair_up(c, cv):
+            slope, bias = sl_t[:, c : c + 1], bias_t[:, c : c + 1]
+            sg2 = keep.tile([P, W], F32, name="sg2_%d" % c)
+            pa2 = keep.tile([P, W], F32, name="pa2_%d" % c)
+            sg = keep.tile([P, W], F32, name="sg_%d" % c)
+            pb2 = keep.tile([P, W], F32, name="pb2_%d" % c)
+            ra = keep.tile([P, W], F32, name="ra%d" % c)
+            rb = keep.tile([P, W], F32, name="rb%d" % c)
+            nc.scalar.activation(sg2[:], cv[:].indirect(n4_t[:]), ACT.Sigmoid, bias=bias, scale=slope)
+            nc.scalar.activation(pa2[:], cv[:].indirect(n3_t[:]), ACT.Copy)
+            nc.gpsimd.tensor_tensor(ra[:], pa2[:], sg2[:], ALU.mult)
+            nc.scalar.activation(sg[:], cv[:].indirect(n3_t[:]), ACT.Sigmoid, bias=bias, scale=slope)
+            nc.scalar.activation(pb2[:], cv[:].indirect(n4_t[:]), ACT.Copy)
+            nc.gpsimd.tensor_tensor(rb[:], pb2[:], sg[:], ALU.subtract)
+            rows = keep.tile([P, N], F32, name="rows%d" % c)
+            nc.scalar.activation(rows[:].indirect(n3_t[:]), ra[:], ACT.Copy)
+            nc.scalar.activation(rows[:].indirect(n4_t[:]), rb[:], ACT.Copy)
+            nc.sync.dma_start(out[c * P : (c + 1) * P, :], rows[:])
+
+        for c in range(BLOCKS):
+            pair_up(c, moments(c))

@@ -40,6 +40,9 @@ def tile_picked_mommedeod_none_p_kernel(tc, x_words, x_scales, wa, wb, gt, gi, s
             nc.sync.dma_start(raw[:], w[:, h * HALF : (h + 1) * HALF].rearrange("(p j) n -> p j n", j=PACK))
             return raw
 
+        warm = keep.tile([P, 1], F32, name="warm")
+        nc.vector.memset(warm[:], 0.0)
+        nc.scalar.activation(warm[:], warm[:], ACT.Sigmoid)
         offs_t = load_list("offs_t", offs)
         two_t = load_list("two_t", two)
         xs = keep.tile([P, T], U8, name="xs")
@@ -101,7 +104,7 @@ def tile_picked_mommedeod_none_p_kernel(tc, x_words, x_scales, wa, wb, gt, gi, s
         wb_codes = [keep.tile([P, HALF], U32, name="wb_codes%d" % h, align_bytes=64) for h in range(2)]
         wb_scales = [keep.tile([P, HALF], U8, name="wb_scales%d" % h, align_bytes=64) for h in range(2)]
 
-        wa_bf = [round_weights("wa_bf0", wa_raw[0], nc.scalar.copy), round_weights("wa_bf1", wa_raw[1], nc.vector.tensor_copy)]
+        wa_bf = [round_weights("wa_bf0", wa_raw[0], nc.scalar.copy), round_weights("wa_bf1", wa_raw[1], nc.scalar.copy)]
         a_ps = [psum.tile([P, H], F32, name="a_ps%d" % t, tag="bank%d" % t) for t in range(PACK)]
         for h in range(2):
             quantise(wa_codes[h][:], wa_scales[h][:], wa_bf[h][:])
@@ -113,9 +116,9 @@ def tile_picked_mommedeod_none_p_kernel(tc, x_words, x_scales, wa, wb, gt, gi, s
                     rhs=wa_codes[h][:].bitcast(FP8X4), rhs_scale=wa_scales[h][:],
                     start=True, stop=True,
                 )
-        xb_w = pick("xb_w", xw[:].bitcast(U32), two_t, U32, tag="wa_bf1")
+        xb_w = pick("xb_w", xw[:].bitcast(U32), two_t, U32, tag="xb")
 
-        wb_bf0 = round_weights("wb_bf0", wb_raw[0], nc.scalar.copy)
+        wb_bf0 = round_weights("wb_bf0", wb_raw[0], nc.vector.tensor_copy)
         a_sb = keep.tile([P, PACK, H], F32, name="a_sb")
         for t in range(PACK):
             if "SSSS"[t] == "S":
@@ -129,7 +132,7 @@ def tile_picked_mommedeod_none_p_kernel(tc, x_words, x_scales, wa, wb, gt, gi, s
         gi_wide = gi_t[:, :, 0:1].unsqueeze(1).to_broadcast([P, P // 4, PACK, 4])
         for h in range(2):
             quantise(wb_codes[h][:], wb_scales[h][:], wb_bf[h][:])
-            z2_bf = keep.tile([P, HALF, PACK], BF16, name="z2_bf%d" % h, align_bytes=64)
+            z2_bf = keep.tile([P, HALF, PACK], BF16, name="z2_bf%d" % h, tag="z2_bf%d" % h, align_bytes=64)
             for u in range(2):
                 b_ps = psum.tile([P, PACK, P], F32, name="b_ps%d" % (2 * h + u), tag="bank%d" % (4 + 2 * h + u))
                 cols = slice(u * P, (u + 1) * P)
@@ -144,7 +147,7 @@ def tile_picked_mommedeod_none_p_kernel(tc, x_words, x_scales, wa, wb, gt, gi, s
             quantise(z2_codes[:, h * HALF : (h + 1) * HALF], z2_scales[:, h * HALF : (h + 1) * HALF], z2_bf[:])
 
         def fetch(engine, dst, window, offsets):
-            if engine == "scalar":
+            if engine == "S":
                 nc.scalar.activation(dst, window.indirect(offsets), ACT.Copy)
             else:
                 nc.vector.tensor_copy(dst, window.indirect(offsets))
@@ -153,16 +156,15 @@ def tile_picked_mommedeod_none_p_kernel(tc, x_words, x_scales, wa, wb, gt, gi, s
             cols = slice(c * P, (c + 1) * P)
             entries = slice(c * LIST_COLS, (c + 1) * LIST_COLS)
 
-            pa = keep.tile([P, PACK, P], F32, name="pa%d" % c, tag="lo%d" % (c - 1 if c > 1 else -1 - c), align_bytes=64)
-            pb = keep.tile([P, PACK, P], F32, name="pb%d" % c, tag="z_codes%d" % (c - 1 if c > 1 else -1 - c), align_bytes=64)
+            pa = keep.tile([P, PACK, P], F32, name="pa%d" % c, tag=["pa0","z2_bf0","z_bf1","z_bf2"][c], align_bytes=64)
+            pb = keep.tile([P, PACK, P], F32, name="pb%d" % c, tag=["pb0","z2_bf1","z_codes1","z_codes2"][c], align_bytes=64)
             for t in range(PACK):
-                engine = "scalar" if "SSSSSSSSVVVVVVVV"[c * PACK + t] == "S" else "vector"
-                fetch(engine, pa[:, t, :], a_sb[:, t, :], n1_t[:, entries])
-                fetch(engine, pb[:, t, :], a_sb[:, t, :], n2_t[:, entries])
-            hi = keep.tile([P, PACK, P], F32, name="hi%d" % c, tag="hi%d" % c, align_bytes=64)
-            lo = keep.tile([P, PACK, P], F32, name="lo%d" % c, tag="lo%d" % c, align_bytes=64)
+                fetch("SSSSSSSSVVVVVVVV"[c * PACK + t], pa[:, t, :], a_sb[:, t, :], n1_t[:, entries])
+                fetch("SSSVSSSSVVVVVVVV"[c * PACK + t], pb[:, t, :], a_sb[:, t, :], n2_t[:, entries])
+            hi = keep.tile([P, PACK, P], F32, name="hi%d" % c, tag=["hi0","z_bf0","hi2","hi3"][c], align_bytes=64)
+            lo = keep.tile([P, PACK, P], F32, name="lo%d" % c, tag=["lo0","z_codes0","lo2","lo3"][c], align_bytes=64)
             mid = keep.tile([P, PACK, P], F32, name="mid%d" % c)
-            step = 4 if c == 0 else PACK
+            step = 2 if c == 0 else PACK
             for t0 in range(0, PACK, step):
                 ts = slice(t0, t0 + step)
                 nc.vector.tensor_tensor(hi[:, ts, :], pa[:, ts, :], pb[:, ts, :], ALU.max)

@@ -61,13 +61,13 @@ def tile_picked_mommedeod_none_p_kernel(tc, x_words, x_scales, wa, wb, gt, gi, s
         sl_t = keep.tile([P, BLOCKS], F32, name="sl_t")
         th_t = keep.tile([P, BLOCKS], F32, name="th_t")
         with nc.allow_non_contiguous_dma(reason="one value a partition and column"):
-            for dst, src, queue in ((gt_t, gt, nc.gpsimd), (gi_t, gi, nc.sync)):
-                for t in range(PACK):
-                    queue.dma_start(dst[:, t, 0:1], src.rearrange("(q t r) o -> t q r o", t=PACK, r=RUN)[t])
-            nc.gpsimd.dma_start(sl_t[:], sl.rearrange("(c p) o -> p (c o)", p=P))
-            nc.gpsimd.dma_start(th_t[:], th.rearrange("(c p) o -> p (c o)", p=P))
+            for dst, src, t in [(gt_t, gt, 0), (gt_t, gt, 1)] + [(gi_t, gi, t) for t in range(PACK)] + [(gt_t, gt, 2), (gt_t, gt, 3)]:
+                nc.gpsimd.dma_start(dst[:, t, 0:1], src.rearrange("(q t r) o -> t q r o", t=PACK, r=RUN)[t])
         n3_t = load_list("n3_t", n3)
         n4_t = load_list("n4_t", n4)
+        with nc.allow_non_contiguous_dma(reason="one value a partition and column"):
+            nc.sync.dma_start(sl_t[:], sl.rearrange("(c p) o -> p (c o)", p=P))
+            nc.sync.dma_start(th_t[:], th.rearrange("(c p) o -> p (c o)", p=P))
         slth = keep.tile([P, BLOCKS], F32, name="slth")
         bias_t = keep.tile([P, BLOCKS], F32, name="bias_t")
         nc.gpsimd.tensor_tensor(slth[:], sl_t[:], th_t[:], ALU.mult)
@@ -101,7 +101,7 @@ def tile_picked_mommedeod_none_p_kernel(tc, x_words, x_scales, wa, wb, gt, gi, s
 
         wa_codes = [keep.tile([P, HALF], U32, name="wa_codes%d" % h, align_bytes=64) for h in range(2)]
         wa_scales = [keep.tile([P, HALF], U8, name="wa_scales%d" % h, align_bytes=64) for h in range(2)]
-        wb_codes = [keep.tile([P, HALF], U32, name="wb_codes%d" % h, align_bytes=64) for h in range(2)]
+        wb_codes = [keep.tile([P, HALF], U32, name="wb_codes%d" % h, tag="wb_codes%d" % h, align_bytes=64) for h in range(2)]
         wb_scales = [keep.tile([P, HALF], U8, name="wb_scales%d" % h, align_bytes=64) for h in range(2)]
 
         wa_bf = [round_weights("wa_bf0", wa_raw[0], nc.scalar.copy), round_weights("wa_bf1", wa_raw[1], nc.scalar.copy)]
@@ -118,13 +118,8 @@ def tile_picked_mommedeod_none_p_kernel(tc, x_words, x_scales, wa, wb, gt, gi, s
                 )
         xb_w = pick("xb_w", xw[:].bitcast(U32), two_t, U32, tag="xb")
 
-        wb_bf0 = round_weights("wb_bf0", wb_raw[0], nc.vector.tensor_copy)
+        wb_bf0 = round_weights("wb_bf0", wb_raw[0], nc.scalar.copy)
         a_sb = keep.tile([P, PACK, H], F32, name="a_sb")
-        for t in range(PACK):
-            if "SSSS"[t] == "S":
-                nc.scalar.activation(a_sb[:, t, :], a_ps[t][:], ACT.Copy, scale=gt_t[:, t, 0:1])
-            else:
-                nc.vector.tensor_scalar(a_sb[:, t, :], a_ps[t][:], gt_t[:, t, 0:1], None, ALU.mult)
         wb_bf = [wb_bf0, round_weights("wb_bf1", wb_raw[1], nc.vector.tensor_copy)]
 
         z2_codes = keep.tile([P, N], U32, name="z2_codes", align_bytes=64)
@@ -132,6 +127,7 @@ def tile_picked_mommedeod_none_p_kernel(tc, x_words, x_scales, wa, wb, gt, gi, s
         gi_wide = gi_t[:, :, 0:1].unsqueeze(1).to_broadcast([P, P // 4, PACK, 4])
         for h in range(2):
             quantise(wb_codes[h][:], wb_scales[h][:], wb_bf[h][:])
+        for h in range(2):
             z2_bf = keep.tile([P, HALF, PACK], BF16, name="z2_bf%d" % h, tag="z2_bf%d" % h, align_bytes=64)
             for u in range(2):
                 b_ps = psum.tile([P, PACK, P], F32, name="b_ps%d" % (2 * h + u), tag="bank%d" % (4 + 2 * h + u))
@@ -156,24 +152,32 @@ def tile_picked_mommedeod_none_p_kernel(tc, x_words, x_scales, wa, wb, gt, gi, s
             cols = slice(c * P, (c + 1) * P)
             entries = slice(c * LIST_COLS, (c + 1) * LIST_COLS)
 
-            pa = keep.tile([P, PACK, P], F32, name="pa%d" % c, tag=["pa0","z2_bf0","z_bf1","z_bf2"][c], align_bytes=64)
-            pb = keep.tile([P, PACK, P], F32, name="pb%d" % c, tag=["pb0","z2_bf1","z_codes1","z_codes2"][c], align_bytes=64)
+            if c == 1:
+                pair = keep.tile([P, 2, PACK, P], F32, name="pair1", tag="z2_bf1", align_bytes=64)
+                pa, pb = pair[:, 0], pair[:, 1]
+            else:
+                pa = keep.tile([P, PACK, P], F32, name="pa%d" % c, tag=["pa0","x","zs0","zs1"][c], align_bytes=64)
+                pb = keep.tile([P, PACK, P], F32, name="pb%d" % c, tag=["pb0","x","z_bf0","hi2"][c], align_bytes=64)
             for t in range(PACK):
+                if c == 0:
+                    nc.scalar.activation(a_sb[:, t, :], a_ps[t][:], ACT.Copy, scale=gt_t[:, t, 0:1])
                 fetch("SSSSSSSSVVVVVVVV"[c * PACK + t], pa[:, t, :], a_sb[:, t, :], n1_t[:, entries])
-                fetch("SSSVSSSSVVVVVVVV"[c * PACK + t], pb[:, t, :], a_sb[:, t, :], n2_t[:, entries])
-            hi = keep.tile([P, PACK, P], F32, name="hi%d" % c, tag=["hi0","z_bf0","hi2","hi3"][c], align_bytes=64)
-            lo = keep.tile([P, PACK, P], F32, name="lo%d" % c, tag=["lo0","z_codes0","lo2","lo3"][c], align_bytes=64)
-            mid = keep.tile([P, PACK, P], F32, name="mid%d" % c)
-            step = 2 if c == 0 else PACK
-            for t0 in range(0, PACK, step):
-                ts = slice(t0, t0 + step)
+                fetch("SSSSSSSSVVVVVVVV"[c * PACK + t], pb[:, t, :], a_sb[:, t, :], n2_t[:, entries])
+            if c == 0:
+                both = keep.tile([P, 2, PACK, P], F32, name="both0", tag="wb_codes1", align_bytes=64)
+                hi, lo = both[:, 0], both[:, 1]
+            else:
+                hi = keep.tile([P, PACK, P], F32, name="hi%d" % c, tag=["hi0","z_bf0","hi2","hi3"][c], align_bytes=64)
+                lo = keep.tile([P, PACK, P], F32, name="lo%d" % c, tag=["lo0","z_codes0","lo2","lo3"][c], align_bytes=64)
+            mid = keep.tile([P, PACK, P], F32, name="mid%d" % c, tag="mid%d" % c, align_bytes=64)
+            for ts in (slice(0, 2), slice(2, 3), slice(3, 4)) if c == 0 else (slice(0, PACK),):
                 nc.vector.tensor_tensor(hi[:, ts, :], pa[:, ts, :], pb[:, ts, :], ALU.max)
                 nc.vector.tensor_tensor(lo[:, ts, :], pa[:, ts, :], pb[:, ts, :], ALU.min)
                 nc.vector.tensor_tensor(mid[:, ts, :], hi[:, ts, :], a_sb[:, ts, cols], ALU.min)
             z_bf = keep.tile([P, P, PACK], BF16, name="z_bf%d" % c, tag="z_bf%d" % c, align_bytes=64)
             nc.vector.tensor_tensor(interleaved(z_bf[:]), planes(lo[:]), planes(mid[:]), ALU.max)
             z_codes = keep.tile([P, P], U32, name="z_codes%d" % c, tag="z_codes%d" % c, align_bytes=64)
-            z_scales = keep.tile([P, P], U8, name="z_scales%d" % c, align_bytes=64)
+            z_scales = keep.tile([P, P], U8, name="z_scales%d" % c, tag="zs%d" % c, align_bytes=64)
             quantise(z_codes[:], z_scales[:], z_bf[:])
             cv_ps = psum.tile([P, N], F32, name="cv_ps%d" % c, tag="bank%d" % c)
             nc.tensor.matmul_mx(

@@ -18,179 +18,195 @@ ACT = mybir.ActivationFunctionType
 P = 128
 PACK = 4
 RUN = 8
+QUADRANT = 32
 HALF = 256
-BLOCKS = 4
+BLOCKS = H // P
 LIST_COLS = P // 16
+LINE = 4
+PAD = 8
+CV_FACTOR = 0.0625
 
 
-def tile_picked_mommedeod_none_p_kernel(tc, x_words, x_scales, wa, wb, gt, gi, sl, th, offs, two, n1, n2, n3, n4, out):
+def tile_picked_mommedeod_none_p_kernel(
+    tc, x_words, x_scales, wa, wb, gt, gi, sl, th, offs, two, n1, n2, n3, n4, out
+):
     nc = tc.nc
     with ExitStack() as ctx:
         lists = ctx.enter_context(tc.tile_pool(name="lists", bufs=1))
         keep = ctx.enter_context(tc.tile_pool(name="keep", bufs=1))
         psum = ctx.enter_context(tc.psum_pool(name="psum", bufs=1))
 
-        def load_list(name, src):
-            t = lists.tile(list(src.shape), U16, name=name)
-            nc.sync.dma_start(t[:], src)
-            return t
-
-        def load_half(name, w, h):
-            raw = keep.tile([P, PACK, HALF], F32, name=name)
-            nc.sync.dma_start(raw[:], w[:, h * HALF : (h + 1) * HALF].rearrange("(p j) n -> p j n", j=PACK))
-            return raw
-
         warm = keep.tile([P, 1], F32, name="warm")
         nc.vector.memset(warm[:], 0.0)
         nc.scalar.activation(warm[:], warm[:], ACT.Sigmoid)
+
+        def load_list(name, src):
+            offsets = lists.tile(list(src.shape), U16, name=name)
+            nc.sync.dma_start(offsets[:], src)
+            return offsets
+
+        def load_half(name, weights, h):
+            raw = keep.tile([P, PACK, HALF], F32, name=name)
+            nc.sync.dma_start(raw[:], weights[:, h * HALF : (h + 1) * HALF].rearrange("(p j) n -> p j n", j=PACK))
+            return raw
+
+        def load_plane(queue, dst, src, t):
+            with nc.allow_non_contiguous_dma(reason="one value a partition"):
+                queue.dma_start(dst[:, t, 0:1], src.rearrange("(g t r) o -> t g r o", t=PACK, r=RUN)[t])
+
+        def load_rows(name, src):
+            dst = keep.tile([P, BLOCKS], F32, name=name)
+            with nc.allow_non_contiguous_dma(reason="one value a partition and block"):
+                nc.sync.dma_start(dst[:], src.rearrange("(c p) o -> p (c o)", p=P))
+            return dst
+
         offs_t = load_list("offs_t", offs)
         two_t = load_list("two_t", two)
         xs = keep.tile([P, T], U8, name="xs")
-        for q in range(4):
-            rows4 = x_scales[0, 4 * q : 4 * q + 4, :].bitcast(I32)
-            nc.sync.dma_start(xs[32 * q : 32 * q + 32, :].bitcast(I32), rows4.unsqueeze(0).to_broadcast([8, 4, T // 4]))
+        for q in range(P // QUADRANT):
+            scale_rows = x_scales[0, 4 * q : 4 * q + 4, :].bitcast(I32)
+            nc.sync.dma_start(
+                xs[QUADRANT * q : QUADRANT * (q + 1), :].bitcast(I32),
+                scale_rows.unsqueeze(0).to_broadcast([QUADRANT // 4, 4, T // 4]),
+            )
         xw = keep.tile([P, T], I32, name="xw")
-        nc.sync.dma_start(xw[:], x_words[0].rearrange("p n t -> p (n t)").bitcast(I32))
+        nc.sync.dma_start(xw[:], x_words[0].rearrange("p n j -> p (n j)").bitcast(I32))
         wa_raw = [load_half("wa_raw%d" % h, wa, h) for h in range(2)]
         wb_raw = [load_half("wb_raw%d" % h, wb, h) for h in range(2)]
         n1_t = load_list("n1_t", n1)
         n2_t = load_list("n2_t", n2)
-
-        gt_t = keep.tile([P, PACK, 8], F32, name="gt_t")
-        gi_t = keep.tile([P, PACK, 8], F32, name="gi_t")
-        sl_t = keep.tile([P, BLOCKS], F32, name="sl_t")
-        th_t = keep.tile([P, BLOCKS], F32, name="th_t")
-        with nc.allow_non_contiguous_dma(reason="one value a partition and column"):
-            for dst, src, t in [(gt_t, gt, 0), (gt_t, gt, 1)] + [(gi_t, gi, t) for t in range(PACK)] + [(gt_t, gt, 2), (gt_t, gt, 3)]:
-                nc.gpsimd.dma_start(dst[:, t, 0:1], src.rearrange("(q t r) o -> t q r o", t=PACK, r=RUN)[t])
+        gt_t = keep.tile([P, PACK, PAD], F32, name="gt_t")
+        gi_t = keep.tile([P, PACK, PAD], F32, name="gi_t")
+        for t in range(PACK // 2):
+            load_plane(nc.gpsimd, gt_t, gt, t)
+        for t in range(PACK):
+            load_plane(nc.gpsimd, gi_t, gi, t)
+        for t in range(PACK // 2, PACK):
+            load_plane(nc.sync, gt_t, gt, t)
         n3_t = load_list("n3_t", n3)
         n4_t = load_list("n4_t", n4)
-        with nc.allow_non_contiguous_dma(reason="one value a partition and column"):
-            nc.sync.dma_start(sl_t[:], sl.rearrange("(c p) o -> p (c o)", p=P))
-            nc.sync.dma_start(th_t[:], th.rearrange("(c p) o -> p (c o)", p=P))
+        sl_t = load_rows("sl_t", sl)
+        th_t = load_rows("th_t", th)
         slth = keep.tile([P, BLOCKS], F32, name="slth")
         bias_t = keep.tile([P, BLOCKS], F32, name="bias_t")
         nc.gpsimd.tensor_tensor(slth[:], sl_t[:], th_t[:], ALU.mult)
         nc.gpsimd.tensor_scalar(bias_t[:], slth[:], -1.0, 0.0, ALU.mult, ALU.add)
 
-        def pick(name, window, offsets, dtype, tag=None):
-            g = keep.tile([P, PACK, P], dtype, name=name, tag=tag or name, align_bytes=64)
-            nc.vector.tensor_copy(g[:].rearrange("p t (q r) -> p q t r", r=RUN), window.indirect(offsets[:]))
-            return g
+        def pick(name, window, offsets, dtype):
+            picked = keep.tile([P, PACK, P], dtype, name=name, align_bytes=64)
+            nc.vector.tensor_copy(picked[:].rearrange("p t (g r) -> p g t r", r=RUN), window.indirect(offsets[:]))
+            return picked
 
-        def interleaved(t):
-            return t.rearrange("p (c i) t -> p c t i", i=4)
+        def from_planes(ap):
+            return ap.rearrange("p t (c i) -> p c t i", i=LINE)
 
-        def planes(t):
-            return t.rearrange("p t (c i) -> p c t i", i=4)
+        def into_words(ap):
+            return ap.rearrange("p (c i) t -> p c t i", i=LINE)
 
         def round_weights(name, raw, copy):
-            g = keep.tile([P, HALF, PACK], BF16, name=name, tag=name, align_bytes=64)
-            copy(interleaved(g[:]), planes(raw[:]))
-            return g
-
-        def gpsimd_round(dst, src):
-            nc.gpsimd.tensor_scalar(dst, src, 1.0, 0.0, ALU.mult, ALU.add)
+            grouped = keep.tile([P, HALF, PACK], BF16, name=name, align_bytes=64)
+            copy(into_words(grouped[:]), from_planes(raw[:]))
+            return grouped
 
         def quantise(codes, scales, grouped):
             nc.vector.quantize_mx(out=codes.bitcast(FP8X4), scales=scales, in_=grouped.rearrange("p n t -> p (n t)"))
 
+        def product(dst, lhs_codes, lhs_scales, rhs_codes, rhs_scales):
+            nc.tensor.matmul_mx(
+                out=dst,
+                lhsT=lhs_codes.bitcast(FP8X4),
+                lhsT_scale=lhs_scales,
+                rhs=rhs_codes.bitcast(FP8X4),
+                rhs_scale=rhs_scales,
+                start=True,
+                stop=True,
+            )
+
+        def slot(name, shape, dtype, tag):
+            return keep.tile(shape, dtype, name=name, tag=tag, align_bytes=64)
+
         xa_s = pick("xa_s", xs[:], offs_t, U8)
         xa_w = pick("xa_w", xw[:].bitcast(U32), offs_t, U32)
         xb_s = pick("xb_s", xs[:], two_t, U8)
-
-        wa_codes = [keep.tile([P, HALF], U32, name="wa_codes%d" % h, align_bytes=64) for h in range(2)]
-        wa_scales = [keep.tile([P, HALF], U8, name="wa_scales%d" % h, align_bytes=64) for h in range(2)]
-        wb_codes = [keep.tile([P, HALF], U32, name="wb_codes%d" % h, tag="wb_codes%d" % h, align_bytes=64) for h in range(2)]
-        wb_scales = [keep.tile([P, HALF], U8, name="wb_scales%d" % h, align_bytes=64) for h in range(2)]
-
-        wa_bf = [round_weights("wa_bf0", wa_raw[0], nc.scalar.copy), round_weights("wa_bf1", wa_raw[1], nc.scalar.copy)]
+        wa_codes = [slot("wa_codes%d" % h, [P, HALF], U32, "wa_codes%d" % h) for h in range(2)]
+        wa_scales = [slot("wa_scales%d" % h, [P, HALF], U8, "wa_scales%d" % h) for h in range(2)]
+        wb_codes = [slot("wb_codes%d" % h, [P, HALF], U32, "wb_codes%d" % h) for h in range(2)]
+        wb_scales = [slot("wb_scales%d" % h, [P, HALF], U8, "wb_scales%d" % h) for h in range(2)]
+        wa_bf = [round_weights("wa_bf%d" % h, wa_raw[h], nc.scalar.copy) for h in range(2)]
         a_ps = [psum.tile([P, H], F32, name="a_ps%d" % t, tag="bank%d" % t) for t in range(PACK)]
         for h in range(2):
             quantise(wa_codes[h][:], wa_scales[h][:], wa_bf[h][:])
         for t in range(PACK):
             for h in range(2):
-                nc.tensor.matmul_mx(
-                    out=a_ps[t][:, h * HALF : (h + 1) * HALF],
-                    lhsT=xa_w[:, t, :].bitcast(FP8X4), lhsT_scale=xa_s[:, t, :],
-                    rhs=wa_codes[h][:].bitcast(FP8X4), rhs_scale=wa_scales[h][:],
-                    start=True, stop=True,
-                )
-        xb_w = pick("xb_w", xw[:].bitcast(U32), two_t, U32, tag="xb")
+                product(a_ps[t][:, h * HALF : (h + 1) * HALF], xa_w[:, t, :], xa_s[:, t, :], wa_codes[h][:], wa_scales[h][:])
 
-        wb_bf0 = round_weights("wb_bf0", wb_raw[0], nc.scalar.copy)
-        a_sb = keep.tile([P, PACK, H], F32, name="a_sb")
-        wb_bf = [wb_bf0, round_weights("wb_bf1", wb_raw[1], nc.vector.tensor_copy)]
-
+        xb_w = pick("xb_w", xw[:].bitcast(U32), two_t, U32)
+        wb_bf = [
+            round_weights("wb_bf0", wb_raw[0], nc.scalar.copy),
+            round_weights("wb_bf1", wb_raw[1], nc.vector.tensor_copy),
+        ]
         z2_codes = keep.tile([P, N], U32, name="z2_codes", align_bytes=64)
         z2_scales = keep.tile([P, N], U8, name="z2_scales", align_bytes=64)
-        gi_wide = gi_t[:, :, 0:1].unsqueeze(1).to_broadcast([P, P // 4, PACK, 4])
+        gi_wide = gi_t[:, :, 0:1].unsqueeze(1).to_broadcast([P, P // LINE, PACK, LINE])
         for h in range(2):
             quantise(wb_codes[h][:], wb_scales[h][:], wb_bf[h][:])
         for h in range(2):
-            z2_bf = keep.tile([P, HALF, PACK], BF16, name="z2_bf%d" % h, tag="z2_bf%d" % h, align_bytes=64)
-            for u in range(2):
-                b_ps = psum.tile([P, PACK, P], F32, name="b_ps%d" % (2 * h + u), tag="bank%d" % (4 + 2 * h + u))
+            z2_bf = slot("z2_bf%d" % h, [P, HALF, PACK], BF16, "z2_bf%d" % h)
+            for u in range(HALF // P):
+                chunk = h * (HALF // P) + u
+                b_ps = psum.tile([P, PACK, P], F32, name="b_ps%d" % chunk, tag="bank%d" % (PACK + chunk))
                 cols = slice(u * P, (u + 1) * P)
                 for t in range(PACK):
-                    nc.tensor.matmul_mx(
-                        out=b_ps[:, t, :],
-                        lhsT=xb_w[:, t, :].bitcast(FP8X4), lhsT_scale=xb_s[:, t, :],
-                        rhs=wb_codes[h][:, cols].bitcast(FP8X4), rhs_scale=wb_scales[h][:, cols],
-                        start=True, stop=True,
-                    )
-                nc.vector.tensor_tensor(interleaved(z2_bf[:, cols, :]), planes(b_ps[:]), gi_wide, ALU.mult)
+                    product(b_ps[:, t, :], xb_w[:, t, :], xb_s[:, t, :], wb_codes[h][:, cols], wb_scales[h][:, cols])
+                nc.vector.tensor_tensor(into_words(z2_bf[:, cols, :]), from_planes(b_ps[:]), gi_wide, ALU.mult)
             quantise(z2_codes[:, h * HALF : (h + 1) * HALF], z2_scales[:, h * HALF : (h + 1) * HALF], z2_bf[:])
 
-        def fetch(engine, dst, window, offsets):
-            if engine == "S":
-                nc.scalar.activation(dst, window.indirect(offsets), ACT.Copy)
-            else:
-                nc.vector.tensor_copy(dst, window.indirect(offsets))
+        ga = keep.tile([P, PACK, H], F32, name="ga")
+
+        def on_scalar(dst, looked_up):
+            nc.scalar.activation(dst, looked_up, ACT.Copy)
+
+        on_vector = nc.vector.tensor_copy
+
+        parts = [
+            [(0, 2, on_scalar, "fetched0a"), (2, 1, on_scalar, "fetched0b"), (3, 1, on_scalar, "fetched0c")],
+            [(0, PACK, on_scalar, "z2_bf1")],
+            [(0, PACK, on_vector, "z2_bf1")],
+            [(0, PACK, on_vector, "z2_bf1")],
+        ]
+        sorted_slots = ["wb_codes1", "z_bf0", "sorted2", "sorted3"]
 
         def moments(c):
             cols = slice(c * P, (c + 1) * P)
             entries = slice(c * LIST_COLS, (c + 1) * LIST_COLS)
-
-            if c == 1:
-                pair = keep.tile([P, 2, PACK, P], F32, name="pair1", tag="z2_bf1", align_bytes=64)
-                pa, pb = pair[:, 0], pair[:, 1]
-            else:
-                pa = keep.tile([P, PACK, P], F32, name="pa%d" % c, tag=["pa0","x","zs0","zs1"][c], align_bytes=64)
-                pb = keep.tile([P, PACK, P], F32, name="pb%d" % c, tag=["pb0","x","z_bf0","hi2"][c], align_bytes=64)
-            for t in range(PACK):
-                if c == 0:
-                    nc.scalar.activation(a_sb[:, t, :], a_ps[t][:], ACT.Copy, scale=gt_t[:, t, 0:1])
-                fetch("SSSSSSSSVVVVVVVV"[c * PACK + t], pa[:, t, :], a_sb[:, t, :], n1_t[:, entries])
-                fetch("SSSSSSSSVVVVVVVV"[c * PACK + t], pb[:, t, :], a_sb[:, t, :], n2_t[:, entries])
-            if c == 0:
-                both = keep.tile([P, 2, PACK, P], F32, name="both0", tag="wb_codes1", align_bytes=64)
-                hi, lo = both[:, 0], both[:, 1]
-            else:
-                hi = keep.tile([P, PACK, P], F32, name="hi%d" % c, tag=["hi0","z_bf0","hi2","hi3"][c], align_bytes=64)
-                lo = keep.tile([P, PACK, P], F32, name="lo%d" % c, tag=["lo0","z_codes0","lo2","lo3"][c], align_bytes=64)
-            mid = keep.tile([P, PACK, P], F32, name="mid%d" % c, tag="mid%d" % c, align_bytes=64)
-            for ts in (slice(0, 2), slice(2, 3), slice(3, 4)) if c == 0 else (slice(0, PACK),):
-                nc.vector.tensor_tensor(hi[:, ts, :], pa[:, ts, :], pb[:, ts, :], ALU.max)
-                nc.vector.tensor_tensor(lo[:, ts, :], pa[:, ts, :], pb[:, ts, :], ALU.min)
-                nc.vector.tensor_tensor(mid[:, ts, :], hi[:, ts, :], a_sb[:, ts, cols], ALU.min)
-            z_bf = keep.tile([P, P, PACK], BF16, name="z_bf%d" % c, tag="z_bf%d" % c, align_bytes=64)
-            nc.vector.tensor_tensor(interleaved(z_bf[:]), planes(lo[:]), planes(mid[:]), ALU.max)
-            z_codes = keep.tile([P, P], U32, name="z_codes%d" % c, tag="z_codes%d" % c, align_bytes=64)
-            z_scales = keep.tile([P, P], U8, name="z_scales%d" % c, tag="zs%d" % c, align_bytes=64)
+            fetched = []
+            for first, count, fetch, tag in parts[c]:
+                pair = slot("pair%d_%d" % (c, first), [P, 2, count, P], F32, tag)
+                for t in range(first, first + count):
+                    if c == 0:
+                        nc.scalar.activation(ga[:, t, :], a_ps[t][:], ACT.Copy, scale=gt_t[:, t, 0:1])
+                    fetch(pair[:, 0, t - first, :], ga[:, t, :].indirect(n1_t[:, entries]))
+                    fetch(pair[:, 1, t - first, :], ga[:, t, :].indirect(n2_t[:, entries]))
+                fetched.append((slice(first, first + count), pair[:, 0], pair[:, 1]))
+            hi_lo = slot("hi_lo%d" % c, [P, 2, PACK, P], F32, sorted_slots[c])
+            hi, lo = hi_lo[:, 0], hi_lo[:, 1]
+            mid = keep.tile([P, PACK, P], F32, name="mid%d" % c)
+            for ts, pa, pb in fetched:
+                nc.vector.tensor_tensor(hi[:, ts, :], pa, pb, ALU.max)
+                nc.vector.tensor_tensor(lo[:, ts, :], pa, pb, ALU.min)
+                nc.vector.tensor_tensor(mid[:, ts, :], hi[:, ts, :], ga[:, ts, cols], ALU.min)
+            z_bf = slot("z_bf%d" % c, [P, P, PACK], BF16, "z_bf%d" % c)
+            nc.vector.tensor_tensor(into_words(z_bf[:]), from_planes(lo), from_planes(mid[:]), ALU.max)
+            z_codes = slot("z_codes%d" % c, [P, P], U32, "z_codes%d" % c)
+            z_scales = keep.tile([P, P], U8, name="z_scales%d" % c, align_bytes=64)
             quantise(z_codes[:], z_scales[:], z_bf[:])
             cv_ps = psum.tile([P, N], F32, name="cv_ps%d" % c, tag="bank%d" % c)
-            nc.tensor.matmul_mx(
-                out=cv_ps[:],
-                lhsT=z_codes[:].bitcast(FP8X4), lhsT_scale=z_scales[:],
-                rhs=z2_codes[:].bitcast(FP8X4), rhs_scale=z2_scales[:],
-                start=True, stop=True,
-            )
-            cv = keep.tile([P, N], F32, name="cv%d" % c)
-            if c < 1:
-                nc.scalar.activation(cv[:], cv_ps[:], ACT.Copy, scale=0.0625)
+            product(cv_ps[:], z_codes[:], z_scales[:], z2_codes[:], z2_scales[:])
+            cv = slot("cv%d" % c, [P, N], F32, "cv%d" % c)
+            if c == 0:
+                nc.scalar.activation(cv[:], cv_ps[:], ACT.Copy, scale=CV_FACTOR)
             else:
-                nc.vector.tensor_scalar(cv[:], cv_ps[:], 0.0625, None, ALU.mult)
+                nc.vector.tensor_scalar(cv[:], cv_ps[:], CV_FACTOR, None, ALU.mult)
             return cv
 
         def pair_up(c, cv):
@@ -200,17 +216,25 @@ def tile_picked_mommedeod_none_p_kernel(tc, x_words, x_scales, wa, wb, gt, gi, s
             sg = keep.tile([P, W], F32, name="sg_%d" % c)
             pb2 = keep.tile([P, W], F32, name="pb2_%d" % c)
             ra = keep.tile([P, W], F32, name="ra%d" % c)
-            rb = keep.tile([P, W], F32, name="rb%d" % c)
+            rows = keep.tile([P, N], F32, name="rows%d" % c)
             nc.scalar.activation(sg2[:], cv[:].indirect(n4_t[:]), ACT.Sigmoid, bias=bias, scale=slope)
             nc.scalar.activation(pa2[:], cv[:].indirect(n3_t[:]), ACT.Copy)
             nc.gpsimd.tensor_tensor(ra[:], pa2[:], sg2[:], ALU.mult)
             nc.scalar.activation(sg[:], cv[:].indirect(n3_t[:]), ACT.Sigmoid, bias=bias, scale=slope)
             nc.scalar.activation(pb2[:], cv[:].indirect(n4_t[:]), ACT.Copy)
-            nc.gpsimd.tensor_tensor(rb[:], pb2[:], sg[:], ALU.subtract)
-            rows = keep.tile([P, N], F32, name="rows%d" % c)
             nc.scalar.activation(rows[:].indirect(n3_t[:]), ra[:], ACT.Copy)
-            nc.scalar.activation(rows[:].indirect(n4_t[:]), rb[:], ACT.Copy)
-            nc.sync.dma_start(out[c * P : (c + 1) * P, :], rows[:])
 
-        for c in range(BLOCKS):
-            pair_up(c, moments(c))
+            def finish(rb_slot):
+                rb = slot("rb%d" % c, [P, W], F32, rb_slot)
+                nc.gpsimd.tensor_tensor(rb[:], pb2[:], sg[:], ALU.subtract)
+                nc.scalar.activation(rows[:].indirect(n4_t[:]), rb[:], ACT.Copy)
+                nc.sync.dma_start(out[c * P : (c + 1) * P, :], rows[:])
+
+            return finish
+
+        for c in range(BLOCKS - 2):
+            pair_up(c, moments(c))("rb%d" % c)
+        finish_second_last = pair_up(BLOCKS - 2, moments(BLOCKS - 2))
+        finish_last = pair_up(BLOCKS - 1, moments(BLOCKS - 1))
+        finish_second_last("cv%d" % (BLOCKS - 1))
+        finish_last("rb%d" % (BLOCKS - 1))

from contextlib import ExitStack

import concourse.mybir as mybir

K, T, S, H, N, W = 512, 2048, 512, 512, 512, 256
FLOPS = 2 * S * K * H + 2 * S * K * N + 2 * H * S * N

F32 = mybir.dt.float32
BF16 = mybir.dt.bfloat16
I32 = mybir.dt.int32
U32 = mybir.dt.uint32
U16 = mybir.dt.uint16
U8 = mybir.dt.uint8
FP8X4 = mybir.dt.float8_e4m3fn_x4
ALU = mybir.AluOpType
ACT = mybir.ActivationFunctionType

P = 128
PACK = 4
RUN = 8
QUADRANT = 32
HALF = 256
BLOCKS = H // P
LIST_COLS = P // 16
LINE = 4
PAD = 8
CV_FACTOR = 0.0625


def tile_picked_mommedeod_none_p_kernel(
    tc, x_words, x_scales, wa, wb, gt, gi, sl, th, offs, two, n1, n2, n3, n4, out
):
    nc = tc.nc
    with ExitStack() as ctx:
        lists = ctx.enter_context(tc.tile_pool(name="lists", bufs=1))
        keep = ctx.enter_context(tc.tile_pool(name="keep", bufs=1))
        psum = ctx.enter_context(tc.psum_pool(name="psum", bufs=1))

        warm = keep.tile([P, 1], F32, name="warm")
        nc.vector.memset(warm[:], 0.0)
        nc.scalar.activation(warm[:], warm[:], ACT.Sigmoid)

        def load_list(name, src):
            offsets = lists.tile(list(src.shape), U16, name=name)
            nc.sync.dma_start(offsets[:], src)
            return offsets

        def load_half(name, weights, h):
            raw = keep.tile([P, PACK, HALF], F32, name=name)
            nc.sync.dma_start(raw[:], weights[:, h * HALF : (h + 1) * HALF].rearrange("(p j) n -> p j n", j=PACK))
            return raw

        def load_plane(queue, dst, src, t):
            with nc.allow_non_contiguous_dma(reason="one value a partition"):
                queue.dma_start(dst[:, t, 0:1], src.rearrange("(g t r) o -> t g r o", t=PACK, r=RUN)[t])

        def load_rows(name, src):
            dst = keep.tile([P, BLOCKS], F32, name=name)
            with nc.allow_non_contiguous_dma(reason="one value a partition and block"):
                nc.sync.dma_start(dst[:], src.rearrange("(c p) o -> p (c o)", p=P))
            return dst

        offs_t = load_list("offs_t", offs)
        two_t = load_list("two_t", two)
        xs = keep.tile([P, T], U8, name="xs")
        for q in range(P // QUADRANT):
            scale_rows = x_scales[0, 4 * q : 4 * q + 4, :].bitcast(I32)
            nc.sync.dma_start(
                xs[QUADRANT * q : QUADRANT * (q + 1), :].bitcast(I32),
                scale_rows.unsqueeze(0).to_broadcast([QUADRANT // 4, 4, T // 4]),
            )
        xw = keep.tile([P, T], I32, name="xw")
        nc.sync.dma_start(xw[:], x_words[0].rearrange("p n j -> p (n j)").bitcast(I32))
        wa_raw = [load_half("wa_raw%d" % h, wa, h) for h in range(2)]
        wb_raw = [load_half("wb_raw%d" % h, wb, h) for h in range(2)]
        n1_t = load_list("n1_t", n1)
        n2_t = load_list("n2_t", n2)
        gt_t = keep.tile([P, PACK, PAD], F32, name="gt_t")
        gi_t = keep.tile([P, PACK, PAD], F32, name="gi_t")
        for t in range(PACK // 2):
            load_plane(nc.gpsimd, gt_t, gt, t)
        for t in range(PACK):
            load_plane(nc.gpsimd, gi_t, gi, t)
        for t in range(PACK // 2, PACK):
            load_plane(nc.sync, gt_t, gt, t)
        n3_t = load_list("n3_t", n3)
        n4_t = load_list("n4_t", n4)
        sl_t = load_rows("sl_t", sl)
        th_t = load_rows("th_t", th)
        slth = keep.tile([P, BLOCKS], F32, name="slth")
        bias_t = keep.tile([P, BLOCKS], F32, name="bias_t")
        nc.gpsimd.tensor_tensor(slth[:], sl_t[:], th_t[:], ALU.mult)
        nc.gpsimd.tensor_scalar(bias_t[:], slth[:], -1.0, 0.0, ALU.mult, ALU.add)

        def pick(name, window, offsets, dtype):
            picked = keep.tile([P, PACK, P], dtype, name=name, align_bytes=64)
            nc.vector.tensor_copy(picked[:].rearrange("p t (g r) -> p g t r", r=RUN), window.indirect(offsets[:]))
            return picked

        def from_planes(ap):
            return ap.rearrange("p t (c i) -> p c t i", i=LINE)

        def into_words(ap):
            return ap.rearrange("p (c i) t -> p c t i", i=LINE)

        def round_weights(name, raw, copy):
            grouped = keep.tile([P, HALF, PACK], BF16, name=name, align_bytes=64)
            copy(into_words(grouped[:]), from_planes(raw[:]))
            return grouped

        def quantise(codes, scales, grouped):
            nc.vector.quantize_mx(out=codes.bitcast(FP8X4), scales=scales, in_=grouped.rearrange("p n t -> p (n t)"))

        def product(dst, lhs_codes, lhs_scales, rhs_codes, rhs_scales):
            nc.tensor.matmul_mx(
                out=dst,
                lhsT=lhs_codes.bitcast(FP8X4),
                lhsT_scale=lhs_scales,
                rhs=rhs_codes.bitcast(FP8X4),
                rhs_scale=rhs_scales,
                start=True,
                stop=True,
            )

        def slot(name, shape, dtype, tag):
            return keep.tile(shape, dtype, name=name, tag=tag, align_bytes=64)

        xa_s = pick("xa_s", xs[:], offs_t, U8)
        xa_w = pick("xa_w", xw[:].bitcast(U32), offs_t, U32)
        xb_s = pick("xb_s", xs[:], two_t, U8)
        wa_codes = [slot("wa_codes%d" % h, [P, HALF], U32, "wa_codes%d" % h) for h in range(2)]
        wa_scales = [slot("wa_scales%d" % h, [P, HALF], U8, "wa_scales%d" % h) for h in range(2)]
        wb_codes = [slot("wb_codes%d" % h, [P, HALF], U32, "wb_codes%d" % h) for h in range(2)]
        wb_scales = [slot("wb_scales%d" % h, [P, HALF], U8, "wb_scales%d" % h) for h in range(2)]
        wa_bf = [round_weights("wa_bf%d" % h, wa_raw[h], nc.scalar.copy) for h in range(2)]
        a_ps = [psum.tile([P, H], F32, name="a_ps%d" % t, tag="bank%d" % t) for t in range(PACK)]
        for h in range(2):
            quantise(wa_codes[h][:], wa_scales[h][:], wa_bf[h][:])
        for t in range(PACK):
            for h in range(2):
                product(a_ps[t][:, h * HALF : (h + 1) * HALF], xa_w[:, t, :], xa_s[:, t, :], wa_codes[h][:], wa_scales[h][:])

        xb_w = pick("xb_w", xw[:].bitcast(U32), two_t, U32)
        wb_bf = [
            round_weights("wb_bf0", wb_raw[0], nc.scalar.copy),
            round_weights("wb_bf1", wb_raw[1], nc.vector.tensor_copy),
        ]
        z2_codes = keep.tile([P, N], U32, name="z2_codes", align_bytes=64)
        z2_scales = keep.tile([P, N], U8, name="z2_scales", align_bytes=64)
        gi_wide = gi_t[:, :, 0:1].unsqueeze(1).to_broadcast([P, P // LINE, PACK, LINE])
        for h in range(2):
            quantise(wb_codes[h][:], wb_scales[h][:], wb_bf[h][:])
        for h in range(2):
            z2_bf = slot("z2_bf%d" % h, [P, HALF, PACK], BF16, "z2_bf%d" % h)
            for u in range(HALF // P):
                chunk = h * (HALF // P) + u
                b_ps = psum.tile([P, PACK, P], F32, name="b_ps%d" % chunk, tag="bank%d" % (PACK + chunk))
                cols = slice(u * P, (u + 1) * P)
                for t in range(PACK):
                    product(b_ps[:, t, :], xb_w[:, t, :], xb_s[:, t, :], wb_codes[h][:, cols], wb_scales[h][:, cols])
                nc.vector.tensor_tensor(into_words(z2_bf[:, cols, :]), from_planes(b_ps[:]), gi_wide, ALU.mult)
            quantise(z2_codes[:, h * HALF : (h + 1) * HALF], z2_scales[:, h * HALF : (h + 1) * HALF], z2_bf[:])

        ga = keep.tile([P, PACK, H], F32, name="ga")

        def on_scalar(dst, looked_up):
            nc.scalar.activation(dst, looked_up, ACT.Copy)

        on_vector = nc.vector.tensor_copy

        parts = [
            [(0, 2, on_scalar, "fetched0a"), (2, 1, on_scalar, "fetched0b"), (3, 1, on_scalar, "fetched0c")],
            [(0, PACK, on_scalar, "z2_bf1")],
            [(0, PACK, on_vector, "z2_bf1")],
            [(0, PACK, on_vector, "z2_bf1")],
        ]
        sorted_slots = ["wb_codes1", "z_bf0", "sorted2", "sorted3"]

        def moments(c):
            cols = slice(c * P, (c + 1) * P)
            entries = slice(c * LIST_COLS, (c + 1) * LIST_COLS)
            fetched = []
            for first, count, fetch, tag in parts[c]:
                pair = slot("pair%d_%d" % (c, first), [P, 2, count, P], F32, tag)
                for t in range(first, first + count):
                    if c == 0:
                        nc.scalar.activation(ga[:, t, :], a_ps[t][:], ACT.Copy, scale=gt_t[:, t, 0:1])
                    fetch(pair[:, 0, t - first, :], ga[:, t, :].indirect(n1_t[:, entries]))
                    fetch(pair[:, 1, t - first, :], ga[:, t, :].indirect(n2_t[:, entries]))
                fetched.append((slice(first, first + count), pair[:, 0], pair[:, 1]))
            hi_lo = slot("hi_lo%d" % c, [P, 2, PACK, P], F32, sorted_slots[c])
            hi, lo = hi_lo[:, 0], hi_lo[:, 1]
            mid = keep.tile([P, PACK, P], F32, name="mid%d" % c)
            for ts, pa, pb in fetched:
                nc.vector.tensor_tensor(hi[:, ts, :], pa, pb, ALU.max)
                nc.vector.tensor_tensor(lo[:, ts, :], pa, pb, ALU.min)
                nc.vector.tensor_tensor(mid[:, ts, :], hi[:, ts, :], ga[:, ts, cols], ALU.min)
            z_bf = slot("z_bf%d" % c, [P, P, PACK], BF16, "z_bf%d" % c)
            nc.vector.tensor_tensor(into_words(z_bf[:]), from_planes(lo), from_planes(mid[:]), ALU.max)
            z_codes = slot("z_codes%d" % c, [P, P], U32, "z_codes%d" % c)
            z_scales = keep.tile([P, P], U8, name="z_scales%d" % c, align_bytes=64)
            quantise(z_codes[:], z_scales[:], z_bf[:])
            cv_ps = psum.tile([P, N], F32, name="cv_ps%d" % c, tag="bank%d" % c)
            product(cv_ps[:], z_codes[:], z_scales[:], z2_codes[:], z2_scales[:])
            cv = slot("cv%d" % c, [P, N], F32, "cv%d" % c)
            if c == 0:
                nc.scalar.activation(cv[:], cv_ps[:], ACT.Copy, scale=CV_FACTOR)
            else:
                nc.vector.tensor_scalar(cv[:], cv_ps[:], CV_FACTOR, None, ALU.mult)
            return cv

        def pair_up(c, cv):
            slope, bias = sl_t[:, c : c + 1], bias_t[:, c : c + 1]
            sg2 = keep.tile([P, W], F32, name="sg2_%d" % c)
            pa2 = keep.tile([P, W], F32, name="pa2_%d" % c)
            sg = keep.tile([P, W], F32, name="sg_%d" % c)
            pb2 = keep.tile([P, W], F32, name="pb2_%d" % c)
            ra = keep.tile([P, W], F32, name="ra%d" % c)
            rows = keep.tile([P, N], F32, name="rows%d" % c)
            nc.scalar.activation(sg2[:], cv[:].indirect(n4_t[:]), ACT.Sigmoid, bias=bias, scale=slope)
            nc.scalar.activation(pa2[:], cv[:].indirect(n3_t[:]), ACT.Copy)
            nc.gpsimd.tensor_tensor(ra[:], pa2[:], sg2[:], ALU.mult)
            nc.scalar.activation(sg[:], cv[:].indirect(n3_t[:]), ACT.Sigmoid, bias=bias, scale=slope)
            nc.scalar.activation(pb2[:], cv[:].indirect(n4_t[:]), ACT.Copy)
            nc.scalar.activation(rows[:].indirect(n3_t[:]), ra[:], ACT.Copy)

            def finish(rb_slot):
                rb = slot("rb%d" % c, [P, W], F32, rb_slot)
                nc.gpsimd.tensor_tensor(rb[:], pb2[:], sg[:], ALU.subtract)
                nc.scalar.activation(rows[:].indirect(n4_t[:]), rb[:], ACT.Copy)
                nc.sync.dma_start(out[c * P : (c + 1) * P, :], rows[:])

            return finish

        for c in range(BLOCKS - 2):
            pair_up(c, moments(c))("rb%d" % c)
        finish_second_last = pair_up(BLOCKS - 2, moments(BLOCKS - 2))
        finish_last = pair_up(BLOCKS - 1, moments(BLOCKS - 1))
        finish_second_last("cv%d" % (BLOCKS - 1))
        finish_last("rb%d" % (BLOCKS - 1))
